import numpy as np
CORES = [48,49,50,51,52,53,54,55,56,57,58,59,60,61,62,63]
N = 16
ROOT = 2
def setup_inputs(rng):
    return {"x": rng.standard_normal((N, 128, N * 256), dtype=np.float32)}
def reference(x):
    return {"y": np.stack([x[ROOT][:, r * 256:(r + 1) * 256] for r in range(N)])}

@@ -1,0 +1,106 @@
+import concourse.bass as bass
+B = 256
+ROOT = 50
+SCRATCH = {'buf': ('sbuf', [128, 16 * B], 'float32'), 'fw': ('sbuf', [128, 4 * B], 'float32'), 'land': ('sbuf', [128, B], 'float32')}
+SEMAPHORES = ['own', 'sent', 'stored', 'ld0', 'ld1', 'ld2', 'ld3', 'ld4', 'ld5', 'ld6', 'ld7', 'grp0', 'grp1', 'grp2', 'grp3']
+
+def sem_table(T):
+    s = T.sem
+    return {'own': s.own, 'sent': s.sent, 'stored': s.stored, 'ld0': s.ld0, 'ld1': s.ld1, 'ld2': s.ld2, 'ld3': s.ld3, 'ld4': s.ld4, 'ld5': s.ld5, 'ld6': s.ld6, 'ld7': s.ld7, 'grp0': s.grp0, 'grp1': s.grp1, 'grp2': s.grp2, 'grp3': s.grp3}
+
+def rng_mask(lo, n):
+    return (1 << n) - 1 << lo
+
+def own(r):
+    return 48 + r
+
+def root_ops():
+    c = own
+    return [('load', 8, 12), ('load', 12, 16), ('send', [(8, [34, c(8)], 0, 4), (9, [c(9)], 4, 4), (10, [54, c(10)], 8, 4), (11, [55, c(11)], 12, 4)]), ('send', [(12, [35, c(12)], 0, 4), (13, [c(13)], 4, 4), (14, [51, c(14)], 8, 4), (15, [54, c(15)], 12, 4)]), ('load', 0, 2), ('load', 3, 8), ('send', [(0, [c(0)], 0, 8), (1, [c(1)], 8, 8)]), ('send', [(4, [c(4)], 0, 4), (5, [c(5)], 4, 4), (6, [c(6)], 8, 4), (7, [c(7)], 12, 4)]), ('send', [(3, [c(3)], 0, 16)]), ('own',)]
+
+def build(topo):
+    acts = {}
+    slots = {}
+    grps = {}
+
+    def add(core, a):
+        acts.setdefault(core, []).append(a)
+
+    def send(src, items):
+        trs = []
+        groups = {}
+        for slot, blk, way, mask in items:
+            nxt = way[0]
+            assert topo.may_write(src, nxt) and mask & ~topo.mask(src, nxt) == 0
+            n = bin(mask).count('1')
+            if len(way) == 1:
+                trs.append((slot, blk, nxt, None, 'own', mask))
+                add(nxt, ('store', n))
+            else:
+                s = slots.get(nxt, 0)
+                slots[nxt] = s + 1
+                if nxt not in groups:
+                    k = grps.get(nxt, 0)
+                    grps[nxt] = k + 1
+                    groups[nxt] = ['grp%d' % k, 0, []]
+                gr = groups[nxt]
+                gr[1] += n
+                gr[2].append((s, blk, way[1:]))
+                trs.append((slot, blk, nxt, s, gr[0], mask))
+        add(src, ('call', trs))
+        for nxt, (sem, total, lst) in groups.items():
+            add(nxt, ('wait', sem, total))
+            width = 16 if all((topo.chip(it[2][0]) == topo.chip(nxt) for it in lst)) else 8
+            per = 1
+            while per * 2 * len(lst) <= width:
+                per *= 2
+            send(nxt, [(it[0], it[1], it[2], rng_mask(i * per, per)) for i, it in enumerate(lst)])
+    loads = []
+    for op in root_ops():
+        if op[0] == 'load':
+            sem = 'ld%d' % len(loads)
+            loads.append([op[1], op[2], sem, False])
+            add(ROOT, ('load', op[1], op[2], sem))
+        elif op[0] == 'send':
+            for ld in loads:
+                if not ld[3] and any((ld[0] <= it[0] < ld[1] for it in op[1])):
+                    ld[3] = True
+                    add(ROOT, ('wait', ld[2], 16))
+            send(ROOT, [(None, b, w, rng_mask(lo, n)) for b, w, lo, n in op[1]])
+        else:
+            add(ROOT, ('own',))
+    return acts
+
+def rank_program(g, core, T, topo):
+    acts = build(topo).get(core)
+    if not acts:
+        return
+    sem = sem_table(T)
+    sent = 0
+    stored = 0
+    for a in acts:
+        if a[0] == 'load':
+            g.dma_start(T.buf[:, a[1] * B:a[2] * B], T.x[:, a[1] * B:a[2] * B]).then_inc(sem[a[3]], 16)
+        elif a[0] == 'wait':
+            g.wait_ge(sem[a[1]], a[2])
+        elif a[0] == 'own':
+            r = T.rank_of(core)
+            g.dma_start(T.y[:], T.x[:, r * B:(r + 1) * B]).then_inc(sem['stored'], 16)
+            stored += 16
+        elif a[0] == 'store':
+            g.wait_ge(sem['own'], a[1])
+            g.dma_start(T.y[:], T.land[:]).then_inc(sem['stored'], 16)
+            stored += 16
+        else:
+            trs = []
+            for slot, blk, nxt, dslot, sname, mask in a[1]:
+                src = T.buf[:, blk * B:(blk + 1) * B] if slot is None else T.fw[:, slot * B:(slot + 1) * B]
+                dst = T.land[:] if dslot is None else T.fw[:, dslot * B:(dslot + 1) * B]
+                rid, pid, se = topo.addr(nxt)
+                trs.append(bass.RemoteDMATransfer(dst_ids=[bass.DstId(rid=rid, pnc=pid)], dma_engine_mask=mask, remote_sem=sem[sname], src=src, dst=dst))
+                sent += bin(mask).count('1')
+            g.remote_dma_fused(trs, local_sem=sem['sent'])
+    if sent:
+        g.wait_ge(sem['sent'], sent)
+    if stored:
+        g.wait_ge(sem['stored'], stored)

@@ -1,30 +1,44 @@
 import concourse.bass as bass
+
 B = 256
 ROOT = 50
-SCRATCH = {'buf': ('sbuf', [128, 16 * B], 'float32'), 'fw': ('sbuf', [128, 4 * B], 'float32'), 'land': ('sbuf', [128, B], 'float32')}
-SEMAPHORES = ['own', 'sent', 'stored', 'ld0', 'ld1', 'ld2', 'ld3', 'ld4', 'ld5', 'ld6', 'ld7', 'grp0', 'grp1', 'grp2', 'grp3']
+SCRATCH = {'buf': ('sbuf', [128, 16 * B], 'float32'),
+           'fw': ('sbuf', [128, 4 * B], 'float32'),
+           'land': ('sbuf', [128, B], 'float32')}
+SEMAPHORES = ['own', 'sent', 'stored', 'gate', 'ld0', 'ld1', 'ld2', 'ld3', 'ld4', 'ld5', 'ld6', 'ld7',
+              'grp0', 'grp1', 'grp2', 'grp3']
 
-def sem_table(T):
-    s = T.sem
-    return {'own': s.own, 'sent': s.sent, 'stored': s.stored, 'ld0': s.ld0, 'ld1': s.ld1, 'ld2': s.ld2, 'ld3': s.ld3, 'ld4': s.ld4, 'ld5': s.ld5, 'ld6': s.ld6, 'ld7': s.ld7, 'grp0': s.grp0, 'grp1': s.grp1, 'grp2': s.grp2, 'grp3': s.grp3}
 
 def rng_mask(lo, n):
     return (1 << n) - 1 << lo
 
+
 def own(r):
     return 48 + r
 
+
 def root_ops():
     c = own
-    return [('load', 8, 12), ('load', 12, 16), ('send', [(8, [34, c(8)], 0, 4), (9, [c(9)], 4, 4), (10, [54, c(10)], 8, 4), (11, [55, c(11)], 12, 4)]), ('send', [(12, [35, c(12)], 0, 4), (13, [c(13)], 4, 4), (14, [51, c(14)], 8, 4), (15, [54, c(15)], 12, 4)]), ('load', 0, 2), ('load', 3, 8), ('send', [(0, [c(0)], 0, 8), (1, [c(1)], 8, 8)]), ('send', [(4, [c(4)], 0, 4), (5, [c(5)], 4, 4), (6, [c(6)], 8, 4), (7, [c(7)], 12, 4)]), ('send', [(3, [c(3)], 0, 16)]), ('own',)]
+    return [
+        ('load', 'sync', 8, 12), ('load', 'scalar', 12, 16),
+        ('send', [(8, [34, c(8)], 0, 4), (9, [c(9)], 4, 4), (10, [54, c(10)], 8, 4), (11, [55, c(11)], 12, 4)]),
+        ('send', [(12, [35, c(12)], 0, 4), (13, [c(13)], 4, 4), (14, [51, c(14)], 8, 4), (15, [54, c(15)], 12, 4)]),
+        ('gate',),
+        ('load', 'sync', 0, 2), ('load', 'scalar', 3, 8),
+        ('send', [(0, [c(0)], 0, 8), (1, [c(1)], 8, 8)]),
+        ('send', [(4, [c(4)], 0, 4), (5, [c(5)], 4, 4), (6, [c(6)], 8, 4), (7, [c(7)], 12, 4)]),
+        ('send', [(3, [c(3)], 0, 16)]),
+        ('own', 'scalar'),
+    ]
+
 
 def build(topo):
     acts = {}
     slots = {}
     grps = {}
 
-    def add(core, a):
-        acts.setdefault(core, []).append(a)
+    def add(core, q, a):
+        acts.setdefault(core, {'g': [], 'sync': [], 'scalar': []})[q].append(a)
 
     def send(src, items):
         trs = []
@@ -35,7 +49,7 @@ def build(topo):
             n = bin(mask).count('1')
             if len(way) == 1:
                 trs.append((slot, blk, nxt, None, 'own', mask))
-                add(nxt, ('store', n))
+                add(nxt, 'sync', ('store', n))
             else:
                 s = slots.get(nxt, 0)
                 slots[nxt] = s + 1
@@ -47,60 +61,80 @@ def build(topo):
                 gr[1] += n
                 gr[2].append((s, blk, way[1:]))
                 trs.append((slot, blk, nxt, s, gr[0], mask))
-        add(src, ('call', trs))
+        add(src, 'g', ('call', trs))
         for nxt, (sem, total, lst) in groups.items():
-            add(nxt, ('wait', sem, total))
-            width = 16 if all((topo.chip(it[2][0]) == topo.chip(nxt) for it in lst)) else 8
+            add(nxt, 'g', ('wait', sem, total))
+            width = 16 if all(topo.chip(it[2][0]) == topo.chip(nxt) for it in lst) else 8
             per = 1
             while per * 2 * len(lst) <= width:
                 per *= 2
             send(nxt, [(it[0], it[1], it[2], rng_mask(i * per, per)) for i, it in enumerate(lst)])
+
     loads = []
+    gates = 0
+    gated = {'sync': 0, 'scalar': 0}
     for op in root_ops():
         if op[0] == 'load':
+            q = op[1]
+            if gated[q] < gates:
+                gated[q] = gates
+                add(ROOT, q, ('wait', 'gate', gates))
             sem = 'ld%d' % len(loads)
-            loads.append([op[1], op[2], sem, False])
-            add(ROOT, ('load', op[1], op[2], sem))
+            loads.append([op[2], op[3], sem, False])
+            add(ROOT, q, ('load', op[2], op[3], sem))
         elif op[0] == 'send':
             for ld in loads:
-                if not ld[3] and any((ld[0] <= it[0] < ld[1] for it in op[1])):
+                if not ld[3] and any(ld[0] <= it[0] < ld[1] for it in op[1]):
                     ld[3] = True
-                    add(ROOT, ('wait', ld[2], 16))
+                    add(ROOT, 'g', ('wait', ld[2], 16))
             send(ROOT, [(None, b, w, rng_mask(lo, n)) for b, w, lo, n in op[1]])
+        elif op[0] == 'gate':
+            gates += 1
+            add(ROOT, 'g', ('inc', 'gate'))
         else:
-            add(ROOT, ('own',))
+            add(ROOT, op[1], ('own',))
     return acts
+
 
 def rank_program(g, core, T, topo):
     acts = build(topo).get(core)
     if not acts:
         return
-    sem = sem_table(T)
-    sent = 0
-    stored = 0
-    for a in acts:
-        if a[0] == 'load':
-            g.dma_start(T.buf[:, a[1] * B:a[2] * B], T.x[:, a[1] * B:a[2] * B]).then_inc(sem[a[3]], 16)
-        elif a[0] == 'wait':
-            g.wait_ge(sem[a[1]], a[2])
-        elif a[0] == 'own':
-            r = T.rank_of(core)
-            g.dma_start(T.y[:], T.x[:, r * B:(r + 1) * B]).then_inc(sem['stored'], 16)
-            stored += 16
-        elif a[0] == 'store':
-            g.wait_ge(sem['own'], a[1])
-            g.dma_start(T.y[:], T.land[:]).then_inc(sem['stored'], 16)
-            stored += 16
-        else:
-            trs = []
-            for slot, blk, nxt, dslot, sname, mask in a[1]:
-                src = T.buf[:, blk * B:(blk + 1) * B] if slot is None else T.fw[:, slot * B:(slot + 1) * B]
-                dst = T.land[:] if dslot is None else T.fw[:, dslot * B:(dslot + 1) * B]
-                rid, pid, se = topo.addr(nxt)
-                trs.append(bass.RemoteDMATransfer(dst_ids=[bass.DstId(rid=rid, pnc=pid)], dma_engine_mask=mask, remote_sem=sem[sname], src=src, dst=dst))
-                sent += bin(mask).count('1')
-            g.remote_dma_fused(trs, local_sem=sem['sent'])
-    if sent:
-        g.wait_ge(sem['sent'], sent)
-    if stored:
-        g.wait_ge(sem['stored'], stored)
+    s = T.sem
+    sem = {'own': s.own, 'sent': s.sent, 'stored': s.stored, 'gate': s.gate, 'ld0': s.ld0, 'ld1': s.ld1,
+           'ld2': s.ld2, 'ld3': s.ld3, 'ld4': s.ld4, 'ld5': s.ld5, 'ld6': s.ld6, 'ld7': s.ld7,
+           'grp0': s.grp0, 'grp1': s.grp1, 'grp2': s.grp2, 'grp3': s.grp3}
+    queues = {'g': g, 'sync': g.sync, 'scalar': g.scalar}
+    for qn in ('sync', 'scalar', 'g'):
+        q = queues[qn]
+        sent = 0
+        stored = 0
+        for a in acts[qn]:
+            if a[0] == 'load':
+                q.dma_start(T.buf[:, a[1] * B:a[2] * B], T.x[:, a[1] * B:a[2] * B]).then_inc(sem[a[3]], 16)
+            elif a[0] == 'wait':
+                q.wait_ge(sem[a[1]], a[2])
+            elif a[0] == 'inc':
+                q.sem_inc(sem[a[1]], 1)
+            elif a[0] == 'own':
+                r = T.rank_of(core)
+                q.dma_start(T.y[:], T.x[:, r * B:(r + 1) * B]).then_inc(sem['stored'], 16)
+                stored += 16
+            elif a[0] == 'store':
+                q.wait_ge(sem['own'], a[1])
+                q.dma_start(T.y[:], T.land[:]).then_inc(sem['stored'], 16)
+                stored += 16
+            else:
+                trs = []
+                for slot, blk, nxt, dslot, sname, mask in a[1]:
+                    src = T.buf[:, blk * B:(blk + 1) * B] if slot is None else T.fw[:, slot * B:(slot + 1) * B]
+                    dst = T.land[:] if dslot is None else T.fw[:, dslot * B:(dslot + 1) * B]
+                    rid, pid, se = topo.addr(nxt)
+                    trs.append(bass.RemoteDMATransfer(dst_ids=[bass.DstId(rid=rid, pnc=pid)], dma_engine_mask=mask,
+                                                      remote_sem=sem[sname], src=src, dst=dst))
+                    sent += bin(mask).count('1')
+                q.remote_dma_fused(trs, local_sem=sem['sent'])
+        if sent:
+            q.wait_ge(sem['sent'], sent)
+        if stored:
+            q.wait_ge(sem['stored'], stored)

@@ -3,7 +3,6 @@ import concourse.bass as bass
 B = 256
 ROOT = 50
 SCRATCH = {'buf': ('sbuf', [128, 16 * B], 'float32'),
-           'fw': ('sbuf', [128, 4 * B], 'float32'),
            'land': ('sbuf', [128, B], 'float32')}
 SEMAPHORES = ['own', 'sent', 'stored', 'gate', 'ld0', 'ld1', 'ld2', 'ld3', 'ld4', 'ld5', 'ld6', 'ld7',
               'grp0', 'grp1', 'grp2', 'grp3']
@@ -13,28 +12,29 @@ def rng_mask(lo, n):
     return (1 << n) - 1 << lo
 
 
-def own(r):
-    return 48 + r
+def fin(b, lo, n):
+    return (b, 1, 48 + b, lo, n, None)
 
 
 def root_ops():
-    c = own
     return [
         ('load', 'sync', 8, 12), ('load', 'scalar', 12, 16),
-        ('send', [(8, [34, c(8)], 0, 4), (9, [c(9)], 4, 4), (10, [54, c(10)], 8, 4), (11, [55, c(11)], 12, 4)]),
-        ('send', [(12, [35, c(12)], 0, 4), (13, [c(13)], 4, 4), (14, [51, c(14)], 8, 4), (15, [54, c(15)], 12, 4)]),
+        ('send', [(8, 2, 51, 0, 8, [(8, 1, 34, 0, 4, [fin(8, 0, 8)]), fin(9, 4, 4)]),
+                  (10, 2, 55, 8, 8, [(10, 1, 38, 0, 4, [fin(10, 0, 8)]), fin(11, 4, 4)])]),
+        ('send', [(12, 2, 51, 0, 8, [fin(12, 0, 4), fin(13, 4, 4)]),
+                  (14, 2, 54, 8, 8, [fin(14, 0, 4), fin(15, 4, 4)])]),
         ('gate',),
-        ('load', 'sync', 0, 2), ('load', 'scalar', 3, 8),
-        ('send', [(0, [c(0)], 0, 8), (1, [c(1)], 8, 8)]),
-        ('send', [(4, [c(4)], 0, 4), (5, [c(5)], 4, 4), (6, [c(6)], 8, 4), (7, [c(7)], 12, 4)]),
-        ('send', [(3, [c(3)], 0, 16)]),
+        ('load', 'sync', 4, 8), ('load', 'scalar', 0, 2), ('load', 'scalar', 3, 4),
+        ('send', [fin(4, 0, 4), fin(5, 4, 4), fin(6, 8, 4), fin(7, 12, 4)]),
+        ('send', [fin(0, 0, 8), fin(1, 8, 8)]),
+        ('send', [fin(3, 0, 16)]),
+        ('gate',),
         ('own', 'scalar'),
     ]
 
 
 def build(topo):
     acts = {}
-    slots = {}
     grps = {}
 
     def add(core, q, a):
@@ -42,52 +42,44 @@ def build(topo):
 
     def send(src, items):
         trs = []
-        groups = {}
-        for slot, blk, way, mask in items:
-            nxt = way[0]
-            assert topo.may_write(src, nxt) and mask & ~topo.mask(src, nxt) == 0
-            n = bin(mask).count('1')
-            if len(way) == 1:
-                trs.append((slot, blk, nxt, None, 'own', mask))
-                add(nxt, 'sync', ('store', n))
+        later = []
+        assert len(set(it[1] for it in items)) == 1
+        for b0, nb, dst, lo, n, sub in items:
+            mask = rng_mask(lo, n)
+            assert topo.may_write(src, dst) and mask & ~topo.mask(src, dst) == 0
+            if sub is None:
+                sem = 'own'
+                add(dst, 'sync', ('store', n))
             else:
-                s = slots.get(nxt, 0)
-                slots[nxt] = s + 1
-                if nxt not in groups:
-                    k = grps.get(nxt, 0)
-                    grps[nxt] = k + 1
-                    groups[nxt] = ['grp%d' % k, 0, []]
-                gr = groups[nxt]
-                gr[1] += n
-                gr[2].append((s, blk, way[1:]))
-                trs.append((slot, blk, nxt, s, gr[0], mask))
+                k = grps.get(dst, 0)
+                grps[dst] = k + 1
+                sem = 'grp%d' % k
+                later.append((dst, sem, n, sub))
+            trs.append((b0, nb, dst, sub is None, sem, mask))
         add(src, 'g', ('call', trs))
-        for nxt, (sem, total, lst) in groups.items():
-            add(nxt, 'g', ('wait', sem, total))
-            width = 16 if all(topo.chip(it[2][0]) == topo.chip(nxt) for it in lst) else 8
-            per = 1
-            while per * 2 * len(lst) <= width:
-                per *= 2
-            send(nxt, [(it[0], it[1], it[2], rng_mask(i * per, per)) for i, it in enumerate(lst)])
+        for dst, sem, n, sub in later:
+            add(dst, 'g', ('wait', sem, n))
+            send(dst, sub)
 
     loads = []
     gates = 0
     gated = {'sync': 0, 'scalar': 0}
     for op in root_ops():
-        if op[0] == 'load':
+        if op[0] in ('load', 'own'):
             q = op[1]
             if gated[q] < gates:
                 gated[q] = gates
                 add(ROOT, q, ('wait', 'gate', gates))
+        if op[0] == 'load':
             sem = 'ld%d' % len(loads)
             loads.append([op[2], op[3], sem, False])
             add(ROOT, q, ('load', op[2], op[3], sem))
         elif op[0] == 'send':
             for ld in loads:
-                if not ld[3] and any(ld[0] <= it[0] < ld[1] for it in op[1]):
+                if not ld[3] and any(it[0] < ld[1] and ld[0] < it[0] + it[1] for it in op[1]):
                     ld[3] = True
                     add(ROOT, 'g', ('wait', ld[2], 16))
-            send(ROOT, [(None, b, w, rng_mask(lo, n)) for b, w, lo, n in op[1]])
+            send(ROOT, op[1])
         elif op[0] == 'gate':
             gates += 1
             add(ROOT, 'g', ('inc', 'gate'))
@@ -126,12 +118,12 @@ def rank_program(g, core, T, topo):
                 stored += 16
             else:
                 trs = []
-                for slot, blk, nxt, dslot, sname, mask in a[1]:
-                    src = T.buf[:, blk * B:(blk + 1) * B] if slot is None else T.fw[:, slot * B:(slot + 1) * B]
-                    dst = T.land[:] if dslot is None else T.fw[:, dslot * B:(dslot + 1) * B]
-                    rid, pid, se = topo.addr(nxt)
+                for b0, nb, dst, final, sname, mask in a[1]:
+                    src = T.buf[:, b0 * B:(b0 + nb) * B]
+                    out = T.land[:] if final else T.buf[:, b0 * B:(b0 + nb) * B]
+                    rid, pid, se = topo.addr(dst)
                     trs.append(bass.RemoteDMATransfer(dst_ids=[bass.DstId(rid=rid, pnc=pid)], dma_engine_mask=mask,
-                                                      remote_sem=sem[sname], src=src, dst=dst))
+                                                      remote_sem=sem[sname], src=src, dst=out))
                     sent += bin(mask).count('1')
                 q.remote_dma_fused(trs, local_sem=sem['sent'])
         if sent:

@@ -1,6 +1,7 @@
 import concourse.bass as bass
 
 B = 256
+H = 128
 ROOT = 50
 SCRATCH = {'buf': ('sbuf', [128, 16 * B], 'float32'),
            'land': ('sbuf', [128, B], 'float32')}
@@ -12,22 +13,34 @@ def rng_mask(lo, n):
     return (1 << n) - 1 << lo
 
 
-def fin(b, lo, n):
-    return (b, 1, 48 + b, lo, n, None)
+def fin(h, nh, lo, n):
+    return (h, nh, 48 + h // 2, lo, n, None)
+
+
+def blk(b, lo, n):
+    return fin(2 * b, 2, lo, n)
+
+
+def hop(h, relay, lo, n):
+    return (h, 1, relay, lo, n, [[fin(h, 1, 0, 8)]])
+
+
+def by_switch(b, near, far, lo, n):
+    return (2 * b, 2, near, lo, n, [[hop(2 * b, far, 0, 8)], [hop(2 * b + 1, far, 0, 8)]])
 
 
 def root_ops():
     return [
         ('load', 'sync', 8, 12), ('load', 'scalar', 12, 16),
-        ('send', [(8, 2, 51, 0, 8, [(8, 1, 34, 0, 4, [fin(8, 0, 8)]), fin(9, 4, 4)]),
-                  (10, 2, 55, 8, 8, [(10, 1, 38, 0, 4, [fin(10, 0, 8)]), fin(11, 4, 4)])]),
-        ('send', [(12, 2, 51, 0, 8, [fin(12, 0, 4), fin(13, 4, 4)]),
-                  (14, 2, 54, 8, 8, [fin(14, 0, 4), fin(15, 4, 4)])]),
+        ('send', [by_switch(8, 49, 34, 0, 4), by_switch(9, 53, 38, 4, 4),
+                  (20, 2, 51, 8, 4, [[blk(10, 0, 8)]]), (22, 2, 55, 12, 4, [[blk(11, 0, 8)]])]),
+        ('send', [(24, 4, 51, 0, 8, [[blk(12, 0, 4), blk(13, 4, 4)]]),
+                  (28, 4, 54, 8, 8, [[blk(14, 0, 4), blk(15, 4, 4)]])]),
         ('gate',),
         ('load', 'sync', 4, 8), ('load', 'scalar', 0, 2), ('load', 'scalar', 3, 4),
-        ('send', [fin(4, 0, 4), fin(5, 4, 4), fin(6, 8, 4), fin(7, 12, 4)]),
-        ('send', [fin(0, 0, 8), fin(1, 8, 8)]),
-        ('send', [fin(3, 0, 16)]),
+        ('send', [blk(4, 0, 4), blk(5, 4, 4), blk(6, 8, 4), blk(7, 12, 4)]),
+        ('send', [blk(0, 0, 8), blk(1, 8, 8)]),
+        ('send', [blk(3, 0, 16)]),
         ('gate',),
         ('own', 'scalar'),
     ]
@@ -36,6 +49,7 @@ def root_ops():
 def build(topo):
     acts = {}
     grps = {}
+    finals = {}
 
     def add(core, q, a):
         acts.setdefault(core, {'g': [], 'sync': [], 'scalar': []})[q].append(a)
@@ -44,22 +58,23 @@ def build(topo):
         trs = []
         later = []
         assert len(set(it[1] for it in items)) == 1
-        for b0, nb, dst, lo, n, sub in items:
+        for h0, nh, dst, lo, n, sub in items:
             mask = rng_mask(lo, n)
             assert topo.may_write(src, dst) and mask & ~topo.mask(src, dst) == 0
             if sub is None:
                 sem = 'own'
-                add(dst, 'sync', ('store', n))
+                finals[dst] = finals.get(dst, 0) + n
             else:
                 k = grps.get(dst, 0)
                 grps[dst] = k + 1
                 sem = 'grp%d' % k
                 later.append((dst, sem, n, sub))
-            trs.append((b0, nb, dst, sub is None, sem, mask))
+            trs.append((h0, nh, dst, sub is None, sem, mask))
         add(src, 'g', ('call', trs))
         for dst, sem, n, sub in later:
             add(dst, 'g', ('wait', sem, n))
-            send(dst, sub)
+            for call in sub:
+                send(dst, call)
 
     loads = []
     gates = 0
@@ -72,7 +87,7 @@ def build(topo):
                 add(ROOT, q, ('wait', 'gate', gates))
         if op[0] == 'load':
             sem = 'ld%d' % len(loads)
-            loads.append([op[2], op[3], sem, False])
+            loads.append([2 * op[2], 2 * op[3], sem, False])
             add(ROOT, q, ('load', op[2], op[3], sem))
         elif op[0] == 'send':
             for ld in loads:
@@ -85,6 +100,8 @@ def build(topo):
             add(ROOT, 'g', ('inc', 'gate'))
         else:
             add(ROOT, op[1], ('own',))
+    for dst, n in finals.items():
+        add(dst, 'sync', ('store', n))
     return acts
 
 
@@ -118,9 +135,10 @@ def rank_program(g, core, T, topo):
                 stored += 16
             else:
                 trs = []
-                for b0, nb, dst, final, sname, mask in a[1]:
-                    src = T.buf[:, b0 * B:(b0 + nb) * B]
-                    out = T.land[:] if final else T.buf[:, b0 * B:(b0 + nb) * B]
+                for h0, nh, dst, final, sname, mask in a[1]:
+                    src = T.buf[:, h0 * H:(h0 + nh) * H]
+                    o = (h0 % 2) * H
+                    out = T.land[:, o:o + nh * H] if final else T.buf[:, h0 * H:(h0 + nh) * H]
                     rid, pid, se = topo.addr(dst)
                     trs.append(bass.RemoteDMATransfer(dst_ids=[bass.DstId(rid=rid, pnc=pid)], dma_engine_mask=mask,
                                                       remote_sem=sem[sname], src=src, dst=out))

import concourse.bass as bass

B = 256
H = 128
ROOT = 50
SCRATCH = {'buf': ('sbuf', [128, 16 * B], 'float32'),
           'land': ('sbuf', [128, B], 'float32')}
SEMAPHORES = ['own', 'sent', 'stored', 'gate', 'ld0', 'ld1', 'ld2', 'ld3', 'ld4', 'ld5', 'ld6', 'ld7',
              'grp0', 'grp1', 'grp2', 'grp3']


def rng_mask(lo, n):
    return (1 << n) - 1 << lo


def fin(h, nh, lo, n):
    return (h, nh, 48 + h // 2, lo, n, None)


def blk(b, lo, n):
    return fin(2 * b, 2, lo, n)


def hop(h, relay, lo, n):
    return (h, 1, relay, lo, n, [[fin(h, 1, 0, 8)]])


def by_switch(b, near, far, lo, n):
    return (2 * b, 2, near, lo, n, [[hop(2 * b, far, 0, 8)], [hop(2 * b + 1, far, 0, 8)]])


def root_ops():
    return [
        ('load', 'sync', 8, 12), ('load', 'scalar', 12, 16),
        ('send', [by_switch(8, 49, 34, 0, 4), by_switch(9, 53, 38, 4, 4),
                  (20, 2, 51, 8, 4, [[blk(10, 0, 8)]]), (22, 2, 55, 12, 4, [[blk(11, 0, 8)]])]),
        ('send', [(24, 4, 51, 0, 8, [[blk(12, 0, 4), blk(13, 4, 4)]]),
                  (28, 4, 54, 8, 8, [[blk(14, 0, 4), blk(15, 4, 4)]])]),
        ('gate',),
        ('load', 'sync', 4, 8), ('load', 'scalar', 0, 2), ('load', 'scalar', 3, 4),
        ('send', [blk(4, 0, 4), blk(5, 4, 4), blk(6, 8, 4), blk(7, 12, 4)]),
        ('send', [blk(0, 0, 8), blk(1, 8, 8)]),
        ('send', [blk(3, 0, 16)]),
        ('gate',),
        ('own', 'scalar'),
    ]


def build(topo):
    acts = {}
    grps = {}
    finals = {}

    def add(core, q, a):
        acts.setdefault(core, {'g': [], 'sync': [], 'scalar': []})[q].append(a)

    def send(src, items):
        trs = []
        later = []
        assert len(set(it[1] for it in items)) == 1
        for h0, nh, dst, lo, n, sub in items:
            mask = rng_mask(lo, n)
            assert topo.may_write(src, dst) and mask & ~topo.mask(src, dst) == 0
            if sub is None:
                sem = 'own'
                finals[dst] = finals.get(dst, 0) + n
            else:
                k = grps.get(dst, 0)
                grps[dst] = k + 1
                sem = 'grp%d' % k
                later.append((dst, sem, n, sub))
            trs.append((h0, nh, dst, sub is None, sem, mask))
        add(src, 'g', ('call', trs))
        for dst, sem, n, sub in later:
            add(dst, 'g', ('wait', sem, n))
            for call in sub:
                send(dst, call)

    loads = []
    gates = 0
    gated = {'sync': 0, 'scalar': 0}
    for op in root_ops():
        if op[0] in ('load', 'own'):
            q = op[1]
            if gated[q] < gates:
                gated[q] = gates
                add(ROOT, q, ('wait', 'gate', gates))
        if op[0] == 'load':
            sem = 'ld%d' % len(loads)
            loads.append([2 * op[2], 2 * op[3], sem, False])
            add(ROOT, q, ('load', op[2], op[3], sem))
        elif op[0] == 'send':
            for ld in loads:
                if not ld[3] and any(it[0] < ld[1] and ld[0] < it[0] + it[1] for it in op[1]):
                    ld[3] = True
                    add(ROOT, 'g', ('wait', ld[2], 16))
            send(ROOT, op[1])
        elif op[0] == 'gate':
            gates += 1
            add(ROOT, 'g', ('inc', 'gate'))
        else:
            add(ROOT, op[1], ('own',))
    for dst, n in finals.items():
        add(dst, 'sync', ('store', n))
    return acts


def rank_program(g, core, T, topo):
    acts = build(topo).get(core)
    if not acts:
        return
    s = T.sem
    sem = {'own': s.own, 'sent': s.sent, 'stored': s.stored, 'gate': s.gate, 'ld0': s.ld0, 'ld1': s.ld1,
           'ld2': s.ld2, 'ld3': s.ld3, 'ld4': s.ld4, 'ld5': s.ld5, 'ld6': s.ld6, 'ld7': s.ld7,
           'grp0': s.grp0, 'grp1': s.grp1, 'grp2': s.grp2, 'grp3': s.grp3}
    queues = {'g': g, 'sync': g.sync, 'scalar': g.scalar}
    for qn in ('sync', 'scalar', 'g'):
        q = queues[qn]
        sent = 0
        stored = 0
        for a in acts[qn]:
            if a[0] == 'load':
                q.dma_start(T.buf[:, a[1] * B:a[2] * B], T.x[:, a[1] * B:a[2] * B]).then_inc(sem[a[3]], 16)
            elif a[0] == 'wait':
                q.wait_ge(sem[a[1]], a[2])
            elif a[0] == 'inc':
                q.sem_inc(sem[a[1]], 1)
            elif a[0] == 'own':
                r = T.rank_of(core)
                q.dma_start(T.y[:], T.x[:, r * B:(r + 1) * B]).then_inc(sem['stored'], 16)
                stored += 16
            elif a[0] == 'store':
                q.wait_ge(sem['own'], a[1])
                q.dma_start(T.y[:], T.land[:]).then_inc(sem['stored'], 16)
                stored += 16
            else:
                trs = []
                for h0, nh, dst, final, sname, mask in a[1]:
                    src = T.buf[:, h0 * H:(h0 + nh) * H]
                    o = (h0 % 2) * H
                    out = T.land[:, o:o + nh * H] if final else T.buf[:, h0 * H:(h0 + nh) * H]
                    rid, pid, se = topo.addr(dst)
                    trs.append(bass.RemoteDMATransfer(dst_ids=[bass.DstId(rid=rid, pnc=pid)], dma_engine_mask=mask,
                                                      remote_sem=sem[sname], src=src, dst=out))
                    sent += bin(mask).count('1')
                q.remote_dma_fused(trs, local_sem=sem['sent'])
        if sent:
            q.wait_ge(sem['sent'], sent)
        if stored:
            q.wait_ge(sem['stored'], stored)
